import numpy as np
import ml_dtypes


def mxq(x, axis, fmt="e4m3"):
    dtype, down = {"e4m3": (ml_dtypes.float8_e4m3fn, 7), "e5m2": (ml_dtypes.float8_e5m2, 14)}[fmt]
    v = np.moveaxis(np.asarray(x, np.float32).astype(ml_dtypes.bfloat16).astype(np.float64), axis, -1)
    blocks = v.reshape(v.shape[:-1] + (-1, 32))
    amax = np.abs(blocks).max(-1, keepdims=True)
    byte = np.maximum(np.where(amax > 0, np.frexp(amax)[1] - 1 + 127, 0) - down, 1)
    scale = np.exp2(byte - 127.0)
    codes = (blocks / scale).astype(np.float32).astype(dtype).astype(np.float64)
    return np.moveaxis((codes * scale).reshape(v.shape), -1, axis)


WIDE = False


def mx_kscale(k):
    if not WIDE:
        return np.ones(k)
    levels = np.array([10, -10, 5, -5, 0])
    if k % 512:
        return np.exp2(np.random.permutation(np.resize(levels, k // 32))).repeat(32)
    a = np.empty((k // 512, 16))
    for p in range(k // 512):
        a[p, :8] = np.random.permutation(np.resize(levels, 8))
        for g in range(8):
            far = levels[np.abs(levels - a[p, g]) >= 10]
            a[p, g + 8] = far[np.random.randint(len(far))]
    return np.exp2(a.ravel()).repeat(32)


def f64(x):
    return np.asarray(x).astype(np.float64)


def striped8(idx):
    return np.concatenate([v.reshape(-1, 16).T for v in idx]).astype(np.uint16)


def unstriped8(offs):
    return np.stack([offs[16 * g:16 * g + 16].T.reshape(-1) for g in range(8)]).astype(np.int64)


E2M1 = np.array([0.0, 0.5, 1.0, 1.5, 2.0, 3.0, 4.0, 6.0, -0.0, -0.5, -1.0, -1.5, -2.0, -3.0, -4.0, -6.0])


def pack_weight(w, fmt):
    k, n = w.shape
    w = f64(np.asarray(w, np.float32).astype(ml_dtypes.bfloat16)).reshape(k // 32, 32, n)
    amax = np.abs(w).max(1)
    if fmt == "e4m3":
        byte = np.frexp(amax)[1] - 1 + 127 - 7
    else:
        mant, ex = np.frexp(amax / 6.0)
        byte = np.where(mant > 0.5, ex, ex - 1) + 127
    byte = np.clip(np.where(amax > 0, byte, 1), 1, 254)
    scaled = (w * np.exp2(127.0 - byte)[:, None, :]).reshape(k, n).astype(np.float32)
    by_word = np.ascontiguousarray(scaled.reshape(k // 512, 128, 4, n).transpose(0, 1, 3, 2))
    if fmt == "e4m3":
        words = by_word.astype(ml_dtypes.float8_e4m3fn).view(np.uint8)
    else:
        c = by_word.astype(ml_dtypes.float4_e2m1fn).view(np.uint8) & 0xF
        words = (c[..., 0::2] | (c[..., 1::2] << 4)).reshape(k // 512, 128, 2 * n)
    return np.ascontiguousarray(words), np.ascontiguousarray(byte.astype(np.uint8).reshape(k // 512, 16, n))


def unpack_weight(words, scales, fmt):
    g, _, n = scales.shape
    words = np.ascontiguousarray(words).reshape(g, 128, n, -1)
    if fmt == "e4m3":
        vals = words.view(ml_dtypes.float8_e4m3fn).astype(np.float64)
    else:
        nib = np.empty((g, 128, n, 4), np.uint8)
        nib[..., 0::2] = words & 0xF
        nib[..., 1::2] = words >> 4
        vals = E2M1[nib]
    vals = vals * np.repeat(np.exp2(scales.astype(np.float64) - 127.0), 8, axis=1)[..., None]
    return vals.transpose(0, 1, 3, 2).reshape(g * 512, n)


K, M, T, S = 2048, 128, 1024, 512


def setup_inputs():
    n = np.random.standard_normal
    s = mx_kscale(K)[:, None]
    p_w = pack_weight(n((K, M)) / np.sqrt(K) / s, "e4m3")
    return {
        "xT": (n((K, T)) * s).astype(np.float32),
        "w_words": p_w[0],
        "w_scales": p_w[1],
        "wgt": np.repeat(np.random.uniform(0.5, 2.0, (8, S)), 16, axis=0).astype(np.float32),
        "r": (n((128, 512))).astype(np.float32),
        "offs": striped8(np.stack([np.random.permutation(T)[:S] for _ in range(8)])),
    }


def reference(xT, w_words, w_scales, wgt, r, offs):
    idx = unstriped8(offs)
    group = np.arange(K) % 512 // 64
    xg = f64(wgt)[np.arange(K) // 4 % 128] * f64(xT)[np.arange(K)[:, None], idx[group]]
    xT_ = mxq(xg, 0, "e4m3")
    w_ = unpack_weight(w_words, w_scales, "e4m3")
    y = w_.T @ xT_
    return f64(r) + y

@@ -1,0 +1,136 @@
+from contextlib import ExitStack
+
+import concourse.mybir as mybir
+
+K, M, T, S = 2048, 128, 1024, 512
+FLOPS = 2 * K * M * S
+
+F32 = mybir.dt.float32
+BF16 = mybir.dt.bfloat16
+I32 = mybir.dt.int32
+U32 = mybir.dt.uint32
+U16 = mybir.dt.uint16
+U8 = mybir.dt.uint8
+FP8X4 = mybir.dt.float8_e4m3fn_x4
+MULT, ADD = mybir.AluOpType.mult, mybir.AluOpType.add
+
+P = 128
+PASSES = K // 512
+CUTS = {0: [(0, 128), (128, 512)], 1: [(0, 128), (128, 512)], 2: [(0, 128), (128, 512)], 3: [(0, 384), (384, 512)]}
+BANKS = [(0, 256), (256, 384), (384, 512)]
+
+
+def tile_list_heads_res_kernel(tc, xT, w_words, w_scales, wgt, r, offs, out):
+    nc = tc.nc
+    with ExitStack() as ctx:
+        keep = ctx.enter_context(tc.tile_pool(name="keep", bufs=1))
+        psum = ctx.enter_context(tc.psum_pool(name="psum", bufs=1))
+
+        lists = keep.tile([P, S // 16], U16, name="lists")
+        factors = keep.tile([P, S], F32, name="factors")
+        nc.scalar.dma_start(out=factors[:, 0:128], in_=wgt[:, 0:128])
+
+        planes = {}
+        for a in range(PASSES):
+            rows = xT[512 * a : 512 * (a + 1), :].rearrange("(p i) t -> p i t", i=4)
+            for i in range(4):
+                planes[a, i] = keep.tile([P, T], F32, name=f"plane{a}_{i}")
+                nc.sync.dma_start(out=planes[a, i][:], in_=rows[:, i, :])
+                if a == 0 and i == 0:
+                    nc.sync.dma_start(lists[:], offs)
+                    nc.sync.dma_start(out=factors[:, 128:512], in_=wgt[:, 128:512])
+
+        w_s = keep.tile([P, PASSES, M], U8, name="w_s", align_bytes=64)
+        nc.vector.memset(w_s[:].rearrange("p a n -> p (a n)").bitcast(I32), 0)
+        for q in range(4):
+            nc.sync.dma_start(
+                out=w_s[32 * q : 32 * q + 4, :, :].bitcast(I32),
+                in_=w_scales[:, 4 * q : 4 * q + 4, :].rearrange("a q n -> q a n").bitcast(I32),
+            )
+        w_c = keep.tile([P, PASSES, M], U32, name="w_c", align_bytes=64)
+        nc.sync.dma_start(
+            out=w_c[:].bitcast(I32),
+            in_=w_words.rearrange("a p n t -> p a (n t)").bitcast(I32),
+        )
+        res = keep.tile([P, S], F32, name="res")
+        nc.sync.dma_start(out=res[:], in_=r)
+
+        picked = {}
+        packed = {}
+        codes = {}
+        scales = {}
+        acc = {}
+        for a in range(PASSES):
+            for c0, c1 in CUTS[a]:
+                picked[a, c0] = keep.tile([P, 4, c1 - c0], F32, name=f"picked{a}_{c0}")
+            packed[a] = keep.tile([P, S, 4], BF16, name=f"packed{a}", align_bytes=64)
+            codes[a] = keep.tile([P, S], U32, name=f"codes{a}", align_bytes=64)
+            scales[a] = keep.tile([P, S], U8, name=f"scales{a}", align_bytes=64)
+        for c0, c1 in BANKS:
+            acc[c0] = psum.tile([M, c1 - c0], F32, name=f"acc{c0}")
+
+        def gather(a, i, c0, c1):
+            nc.vector.tensor_tensor(
+                picked[a, c0][:, i, :],
+                planes[a, i][:].indirect(lists[:, c0 // 16 : c1 // 16]),
+                factors[:, c0:c1],
+                MULT,
+            )
+
+        def interleave(copy, a, c0, c1):
+            p0 = max(start for start, stop in CUTS[a] if start <= c0)
+            copy(
+                out=packed[a][:, c0:c1, :].rearrange("p (c i) t -> p c t i", i=4),
+                in_=picked[a, p0][:, :, c0 - p0 : c1 - p0].rearrange("p t (c i) -> p c t i", i=4),
+            )
+
+        def quantize(a, c0, c1):
+            nc.vector.quantize_mx(
+                out=codes[a][:, c0:c1].bitcast(FP8X4),
+                scales=scales[a][:, c0:c1],
+                in_=packed[a][:, c0:c1, :].rearrange("p c t -> p (c t)"),
+            )
+
+        def multiply(a, c0, c1):
+            nc.tensor.matmul_mx(
+                out=acc[c0][:],
+                lhsT=w_c[:, a, :].bitcast(FP8X4),
+                lhsT_scale=w_s[:, a, :],
+                rhs=codes[a][:, c0:c1].bitcast(FP8X4),
+                rhs_scale=scales[a][:, c0:c1],
+                start=(a == 0),
+                stop=(a == PASSES - 1),
+            )
+
+        def finish(c0, c1):
+            done = keep.tile([M, c1 - c0], F32, name=f"done{c0}")
+            nc.vector.tensor_tensor(done[:], acc[c0][:], res[:, c0:c1], ADD)
+            nc.sync.dma_start(out=out[:, c0:c1], in_=done[:])
+
+        for a in range(PASSES - 1):
+            for i in range(4):
+                for c0, c1 in CUTS[a]:
+                    gather(a, i, c0, c1)
+                if a > 0 and i == 2:
+                    quantize(a - 1, 0, S)
+            for c0, c1 in CUTS[a]:
+                interleave(nc.scalar.copy, a, c0, c1)
+        for i in range(3):
+            gather(3, i, 0, 384)
+            gather(3, i, 384, 512)
+        quantize(2, 0, S)
+        for a in range(PASSES - 1):
+            for c0, c1 in BANKS:
+                multiply(a, c0, c1)
+        gather(3, 3, 0, 384)
+        interleave(nc.scalar.copy, 3, 0, 256)
+        gather(3, 3, 384, 512)
+        interleave(nc.vector.tensor_copy, 3, 256, 384)
+        interleave(nc.vector.tensor_copy, 3, 384, 448)
+        interleave(nc.scalar.copy, 3, 448, 512)
+        ends = [BANKS[1], BANKS[0], BANKS[2]]
+        for c0, c1 in ends:
+            quantize(3, c0, c1)
+            multiply(3, c0, c1)
+        for c0, c1 in ends:
+            finish(c0, c1)

@@ -16,8 +16,9 @@ MULT, ADD = mybir.AluOpType.mult, mybir.AluOpType.add
 
 P = 128
 PASSES = K // 512
-CUTS = {0: [(0, 128), (128, 512)], 1: [(0, 128), (128, 512)], 2: [(0, 128), (128, 512)], 3: [(0, 384), (384, 512)]}
-BANKS = [(0, 256), (256, 384), (384, 512)]
+LAST = PASSES - 1
+Q = 128
+BANKS = [(0, 128), (128, 256), (256, 384), (384, 512)]
 
 
 def tile_list_heads_res_kernel(tc, xT, w_words, w_scales, wgt, r, offs, out):
@@ -28,17 +29,17 @@ def tile_list_heads_res_kernel(tc, xT, w_words, w_scales, wgt, r, offs, out):
 
         lists = keep.tile([P, S // 16], U16, name="lists")
         factors = keep.tile([P, S], F32, name="factors")
-        nc.scalar.dma_start(out=factors[:, 0:128], in_=wgt[:, 0:128])
+        nc.scalar.dma_start(out=factors[:, 0:Q], in_=wgt[:, 0:Q])
 
         planes = {}
         for a in range(PASSES):
             rows = xT[512 * a : 512 * (a + 1), :].rearrange("(p i) t -> p i t", i=4)
             for i in range(4):
-                planes[a, i] = keep.tile([P, T], F32, name=f"plane{a}_{i}")
+                planes[a, i] = keep.tile([P, T], F32, name=f"plane{a}_{i}", tag=f"plane{a}_{i}", align_bytes=64)
                 nc.sync.dma_start(out=planes[a, i][:], in_=rows[:, i, :])
                 if a == 0 and i == 0:
                     nc.sync.dma_start(lists[:], offs)
-                    nc.sync.dma_start(out=factors[:, 128:512], in_=wgt[:, 128:512])
+                    nc.sync.dma_start(out=factors[:, Q:S], in_=wgt[:, Q:S])
 
         w_s = keep.tile([P, PASSES, M], U8, name="w_s", align_bytes=64)
         nc.vector.memset(w_s[:].rearrange("p a n -> p (a n)").bitcast(I32), 0)
@@ -55,33 +56,32 @@ def tile_list_heads_res_kernel(tc, xT, w_words, w_scales, wgt, r, offs, out):
         res = keep.tile([P, S], F32, name="res")
         nc.sync.dma_start(out=res[:], in_=r)
 
-        picked = {}
-        packed = {}
-        codes = {}
-        scales = {}
-        acc = {}
-        for a in range(PASSES):
-            for c0, c1 in CUTS[a]:
-                picked[a, c0] = keep.tile([P, 4, c1 - c0], F32, name=f"picked{a}_{c0}")
-            packed[a] = keep.tile([P, S, 4], BF16, name=f"packed{a}", align_bytes=64)
-            codes[a] = keep.tile([P, S], U32, name=f"codes{a}", align_bytes=64)
-            scales[a] = keep.tile([P, S], U8, name=f"scales{a}", align_bytes=64)
-        for c0, c1 in BANKS:
-            acc[c0] = psum.tile([M, c1 - c0], F32, name=f"acc{c0}")
+        picked = {a: keep.tile([P, 4, S], F32, name=f"picked{a}") for a in range(LAST)}
+        front_packed = keep.tile([P, 2 * S, 4], BF16, name="front_packed", align_bytes=64)
+        front_codes = keep.tile([P, 2 * S], U32, name="front_codes", align_bytes=64)
+        front_scales = keep.tile([P, 2 * S], U8, name="front_scales", align_bytes=64)
+        picked[LAST] = keep.tile([P, 4, S], F32, name="picked_last")
+        packed = {0: front_packed[:, 0:S, :], 1: front_packed[:, S : 2 * S, :]}
+        codes = {0: front_codes[:, 0:S], 1: front_codes[:, S : 2 * S]}
+        scales = {0: front_scales[:, 0:S], 1: front_scales[:, S : 2 * S]}
+        for a in (2, 3):
+            packed[a] = keep.tile([P, S, 4], BF16, name=f"packed{a}", align_bytes=64)[:]
+            scales[a] = keep.tile([P, S], U8, name=f"scales{a}", align_bytes=64)[:]
+        codes[3] = keep.tile([P, S], U32, name="codes3", align_bytes=64)[:]
+        acc = {c0: psum.tile([M, c1 - c0], F32, name=f"acc{c0}") for c0, c1 in BANKS}
 
         def gather(a, i, c0, c1):
             nc.vector.tensor_tensor(
-                picked[a, c0][:, i, :],
+                picked[a][:, i, c0:c1],
                 planes[a, i][:].indirect(lists[:, c0 // 16 : c1 // 16]),
                 factors[:, c0:c1],
                 MULT,
             )
 
         def interleave(copy, a, c0, c1):
-            p0 = max(start for start, stop in CUTS[a] if start <= c0)
             copy(
                 out=packed[a][:, c0:c1, :].rearrange("p (c i) t -> p c t i", i=4),
-                in_=picked[a, p0][:, :, c0 - p0 : c1 - p0].rearrange("p t (c i) -> p c t i", i=4),
+                in_=picked[a][:, :, c0:c1].rearrange("p t (c i) -> p c t i", i=4),
             )
 
         def quantize(a, c0, c1):
@@ -99,7 +99,7 @@ def tile_list_heads_res_kernel(tc, xT, w_words, w_scales, wgt, r, offs, out):
                 rhs=codes[a][:, c0:c1].bitcast(FP8X4),
                 rhs_scale=scales[a][:, c0:c1],
                 start=(a == 0),
-                stop=(a == PASSES - 1),
+                stop=(a == LAST),
             )
 
         def finish(c0, c1):
@@ -107,30 +107,42 @@ def tile_list_heads_res_kernel(tc, xT, w_words, w_scales, wgt, r, offs, out):
             nc.vector.tensor_tensor(done[:], acc[c0][:], res[:, c0:c1], ADD)
             nc.sync.dma_start(out=out[:, c0:c1], in_=done[:])
 
-        for a in range(PASSES - 1):
-            for i in range(4):
-                for c0, c1 in CUTS[a]:
-                    gather(a, i, c0, c1)
-                if a > 0 and i == 2:
-                    quantize(a - 1, 0, S)
-            for c0, c1 in CUTS[a]:
-                interleave(nc.scalar.copy, a, c0, c1)
+        gather(0, 0, 0, Q)
+        gather(0, 0, Q, S)
+        for i in range(1, 4):
+            gather(0, i, 0, S)
+        interleave(nc.scalar.copy, 0, 0, S)
         for i in range(3):
-            gather(3, i, 0, 384)
-            gather(3, i, 384, 512)
-        quantize(2, 0, S)
-        for a in range(PASSES - 1):
+            gather(1, i, 0, S)
+        for c0, c1 in ((0, S // 2), (S // 2, S)):
+            gather(1, 3, c0, c1)
+            interleave(nc.scalar.copy, 1, c0, c1)
+        for i in range(4):
+            gather(2, i, 0, S)
+            if i == 1:
+                nc.vector.quantize_mx(
+                    out=front_codes[:].bitcast(FP8X4),
+                    scales=front_scales[:],
+                    in_=front_packed[:].rearrange("p c t -> p (c t)"),
+                )
+        interleave(nc.scalar.copy, 2, 0, S)
+        for a in range(2):
             for c0, c1 in BANKS:
                 multiply(a, c0, c1)
-        gather(3, 3, 0, 384)
-        interleave(nc.scalar.copy, 3, 0, 256)
-        gather(3, 3, 384, 512)
-        interleave(nc.vector.tensor_copy, 3, 256, 384)
-        interleave(nc.vector.tensor_copy, 3, 384, 448)
-        interleave(nc.scalar.copy, 3, 448, 512)
-        ends = [BANKS[1], BANKS[0], BANKS[2]]
-        for c0, c1 in ends:
-            quantize(3, c0, c1)
-            multiply(3, c0, c1)
-        for c0, c1 in ends:
+        for i in range(3):
+            gather(LAST, i, 0, S)
+        for c0, c1 in BANKS:
+            gather(LAST, 3, c0, c1)
+            interleave(nc.scalar.copy, LAST, c0, min(c1, S - 64))
+        codes[2] = keep.tile([P, S], U32, name="codes2", tag="plane3_3", align_bytes=64)[:]
+        quantize(LAST, *BANKS[0])
+        quantize(2, 0, S)
+        interleave(nc.vector.tensor_copy, LAST, S - 64, S)
+        for c0, c1 in BANKS:
+            multiply(2, c0, c1)
+        multiply(LAST, *BANKS[0])
+        for c0, c1 in BANKS[1:]:
+            quantize(LAST, c0, c1)
+            multiply(LAST, c0, c1)
+        for c0, c1 in BANKS:
             finish(c0, c1)

@@ -28,14 +28,16 @@ def tile_list_heads_res_kernel(tc, xT, w_words, w_scales, wgt, r, offs, out):
         psum = ctx.enter_context(tc.psum_pool(name="psum", bufs=1))
 
         lists = keep.tile([P, S // 16], U16, name="lists")
+        first = keep.tile([P, Q], F32, name="first", tag="first", align_bytes=64)
         factors = keep.tile([P, S], F32, name="factors")
-        nc.scalar.dma_start(out=factors[:, 0:Q], in_=wgt[:, 0:Q])
+        nc.scalar.dma_start(out=first[:], in_=wgt[:, 0:Q])
+        nc.scalar.copy(out=factors[:, 0:Q], in_=first[:])
 
         planes = {}
         for a in range(PASSES):
             rows = xT[512 * a : 512 * (a + 1), :].rearrange("(p i) t -> p i t", i=4)
             for i in range(4):
-                planes[a, i] = keep.tile([P, T], F32, name=f"plane{a}_{i}", tag=f"plane{a}_{i}", align_bytes=64)
+                planes[a, i] = keep.tile([P, T], F32, name=f"plane{a}_{i}")
                 nc.sync.dma_start(out=planes[a, i][:], in_=rows[:, i, :])
                 if a == 0 and i == 0:
                     nc.sync.dma_start(lists[:], offs)
@@ -60,28 +62,33 @@ def tile_list_heads_res_kernel(tc, xT, w_words, w_scales, wgt, r, offs, out):
         front_packed = keep.tile([P, 2 * S, 4], BF16, name="front_packed", align_bytes=64)
         front_codes = keep.tile([P, 2 * S], U32, name="front_codes", align_bytes=64)
         front_scales = keep.tile([P, 2 * S], U8, name="front_scales", align_bytes=64)
-        picked[LAST] = keep.tile([P, 4, S], F32, name="picked_last")
+        picked[LAST] = keep.tile([P, 4, S - Q], F32, name="picked_last", tag="picked_last", align_bytes=64)
         packed = {0: front_packed[:, 0:S, :], 1: front_packed[:, S : 2 * S, :]}
         codes = {0: front_codes[:, 0:S], 1: front_codes[:, S : 2 * S]}
         scales = {0: front_scales[:, 0:S], 1: front_scales[:, S : 2 * S]}
         for a in (2, 3):
             packed[a] = keep.tile([P, S, 4], BF16, name=f"packed{a}", align_bytes=64)[:]
-            scales[a] = keep.tile([P, S], U8, name=f"scales{a}", align_bytes=64)[:]
-        codes[3] = keep.tile([P, S], U32, name="codes3", align_bytes=64)[:]
+            codes[a] = keep.tile([P, S], U32, name=f"codes{a}", align_bytes=64)[:]
+        scales[3] = keep.tile([P, S], U8, name="scales3", align_bytes=64)[:]
         acc = {c0: psum.tile([M, c1 - c0], F32, name=f"acc{c0}") for c0, c1 in BANKS}
+
+        def rows_of(a, c0, c1):
+            if a == LAST and c0 == S - Q:
+                return picked["end"][:]
+            return picked[a][:, :, c0:c1]
 
         def gather(a, i, c0, c1):
             nc.vector.tensor_tensor(
-                picked[a][:, i, c0:c1],
+                rows_of(a, c0, c1)[:, i, :],
                 planes[a, i][:].indirect(lists[:, c0 // 16 : c1 // 16]),
-                factors[:, c0:c1],
+                first[:] if c1 == Q else factors[:, c0:c1],
                 MULT,
             )
 
         def interleave(copy, a, c0, c1):
             copy(
                 out=packed[a][:, c0:c1, :].rearrange("p (c i) t -> p c t i", i=4),
-                in_=picked[a][:, :, c0:c1].rearrange("p t (c i) -> p c t i", i=4),
+                in_=rows_of(a, c0, c1).rearrange("p t (c i) -> p c t i", i=4),
             )
 
         def quantize(a, c0, c1):
@@ -91,7 +98,7 @@ def tile_list_heads_res_kernel(tc, xT, w_words, w_scales, wgt, r, offs, out):
                 in_=packed[a][:, c0:c1, :].rearrange("p c t -> p (c t)"),
             )
 
-        def multiply(a, c0, c1):
+        def multiply(a, c0, c1, stop):
             nc.tensor.matmul_mx(
                 out=acc[c0][:],
                 lhsT=w_c[:, a, :].bitcast(FP8X4),
@@ -99,13 +106,12 @@ def tile_list_heads_res_kernel(tc, xT, w_words, w_scales, wgt, r, offs, out):
                 rhs=codes[a][:, c0:c1].bitcast(FP8X4),
                 rhs_scale=scales[a][:, c0:c1],
                 start=(a == 0),
-                stop=(a == LAST),
+                stop=stop,
             )
 
         def finish(c0, c1):
-            done = keep.tile([M, c1 - c0], F32, name=f"done{c0}")
-            nc.vector.tensor_tensor(done[:], acc[c0][:], res[:, c0:c1], ADD)
-            nc.sync.dma_start(out=out[:, c0:c1], in_=done[:])
+            nc.vector.tensor_tensor(done[:, c0:c1], acc[c0][:], res[:, c0:c1], ADD)
+            nc.sync.dma_start(out=out[:, c0:c1], in_=done[:, c0:c1])
 
         gather(0, 0, 0, Q)
         gather(0, 0, Q, S)
@@ -128,21 +134,30 @@ def tile_list_heads_res_kernel(tc, xT, w_words, w_scales, wgt, r, offs, out):
         interleave(nc.scalar.copy, 2, 0, S)
         for a in range(2):
             for c0, c1 in BANKS:
-                multiply(a, c0, c1)
+                multiply(a, c0, c1, False)
         for i in range(3):
-            gather(LAST, i, 0, S)
-        for c0, c1 in BANKS:
+            gather(LAST, i, 0, S - Q)
+        for c0, c1 in ((0, Q), (Q, S - Q)):
             gather(LAST, 3, c0, c1)
-            interleave(nc.scalar.copy, LAST, c0, min(c1, S - 64))
-        codes[2] = keep.tile([P, S], U32, name="codes2", tag="plane3_3", align_bytes=64)[:]
-        quantize(LAST, *BANKS[0])
-        quantize(2, 0, S)
-        interleave(nc.vector.tensor_copy, LAST, S - 64, S)
-        for c0, c1 in BANKS:
-            multiply(2, c0, c1)
-        multiply(LAST, *BANKS[0])
-        for c0, c1 in BANKS[1:]:
-            quantize(LAST, c0, c1)
-            multiply(LAST, c0, c1)
+            interleave(nc.scalar.copy, LAST, c0, c1)
+        picked["end"] = keep.tile([P, 4, Q], F32, name="picked_end", tag="first", align_bytes=64)
+        for i in range(4):
+            gather(LAST, i, S - Q, S)
+        interleave(nc.scalar.copy, LAST, S - Q, S)
+        scales[2] = keep.tile([P, S], U8, name="scales2", tag="picked_last", align_bytes=64)[:]
+        quantize(LAST, 0, Q)
+        multiply(LAST, *BANKS[0], False)
+        quantize(2, 0, S // 2)
+        multiply(2, *BANKS[0], True)
+        multiply(2, *BANKS[1], False)
+        quantize(LAST, Q, S - Q)
+        multiply(LAST, *BANKS[1], True)
+        multiply(LAST, *BANKS[2], False)
+        quantize(2, S // 2, S)
+        multiply(2, *BANKS[2], True)
+        multiply(2, *BANKS[3], False)
+        quantize(LAST, S - Q, S)
+        multiply(LAST, *BANKS[3], True)
+        done = keep.tile([M, S], F32, name="done", tag="first", align_bytes=64)
         for c0, c1 in BANKS:
             finish(c0, c1)

@@ -25,10 +25,11 @@ def tile_list_heads_res_kernel(tc, xT, w_words, w_scales, wgt, r, offs, out):
     nc = tc.nc
     with ExitStack() as ctx:
         keep = ctx.enter_context(tc.tile_pool(name="keep", bufs=1))
+        late = ctx.enter_context(tc.tile_pool(name="late", bufs=1))
         psum = ctx.enter_context(tc.psum_pool(name="psum", bufs=1))
 
         lists = keep.tile([P, S // 16], U16, name="lists")
-        first = keep.tile([P, Q], F32, name="first", tag="first", align_bytes=64)
+        first = late.tile([P, Q], F32, name="first", align_bytes=64, offset=768)
         factors = keep.tile([P, S], F32, name="factors")
         nc.scalar.dma_start(out=first[:], in_=wgt[:, 0:Q])
         nc.scalar.copy(out=factors[:, 0:Q], in_=first[:])
@@ -61,25 +62,19 @@ def tile_list_heads_res_kernel(tc, xT, w_words, w_scales, wgt, r, offs, out):
         picked = {a: keep.tile([P, 4, S], F32, name=f"picked{a}") for a in range(LAST)}
         front_packed = keep.tile([P, 2 * S, 4], BF16, name="front_packed", align_bytes=64)
         front_codes = keep.tile([P, 2 * S], U32, name="front_codes", align_bytes=64)
-        front_scales = keep.tile([P, 2 * S], U8, name="front_scales", align_bytes=64)
-        picked[LAST] = keep.tile([P, 4, S - Q], F32, name="picked_last", tag="picked_last", align_bytes=64)
+        picked[LAST] = keep.tile([P, 4, S], F32, name="picked_last", tag="picked_last")
         packed = {0: front_packed[:, 0:S, :], 1: front_packed[:, S : 2 * S, :]}
         codes = {0: front_codes[:, 0:S], 1: front_codes[:, S : 2 * S]}
-        scales = {0: front_scales[:, 0:S], 1: front_scales[:, S : 2 * S]}
+        scales = {}
         for a in (2, 3):
             packed[a] = keep.tile([P, S, 4], BF16, name=f"packed{a}", align_bytes=64)[:]
             codes[a] = keep.tile([P, S], U32, name=f"codes{a}", align_bytes=64)[:]
         scales[3] = keep.tile([P, S], U8, name="scales3", align_bytes=64)[:]
         acc = {c0: psum.tile([M, c1 - c0], F32, name=f"acc{c0}") for c0, c1 in BANKS}
 
-        def rows_of(a, c0, c1):
-            if a == LAST and c0 == S - Q:
-                return picked["end"][:]
-            return picked[a][:, :, c0:c1]
-
         def gather(a, i, c0, c1):
             nc.vector.tensor_tensor(
-                rows_of(a, c0, c1)[:, i, :],
+                picked[a][:, i, c0:c1],
                 planes[a, i][:].indirect(lists[:, c0 // 16 : c1 // 16]),
                 first[:] if c1 == Q else factors[:, c0:c1],
                 MULT,
@@ -88,7 +83,7 @@ def tile_list_heads_res_kernel(tc, xT, w_words, w_scales, wgt, r, offs, out):
         def interleave(copy, a, c0, c1):
             copy(
                 out=packed[a][:, c0:c1, :].rearrange("p (c i) t -> p c t i", i=4),
-                in_=rows_of(a, c0, c1).rearrange("p t (c i) -> p c t i", i=4),
+                in_=picked[a][:, :, c0:c1].rearrange("p t (c i) -> p c t i", i=4),
             )
 
         def quantize(a, c0, c1):
@@ -118,33 +113,26 @@ def tile_list_heads_res_kernel(tc, xT, w_words, w_scales, wgt, r, offs, out):
         for i in range(1, 4):
             gather(0, i, 0, S)
         interleave(nc.scalar.copy, 0, 0, S)
+        for a in (1, 2):
+            for i in range(4):
+                gather(a, i, 0, S)
+            interleave(nc.scalar.copy, a, 0, S)
         for i in range(3):
-            gather(1, i, 0, S)
-        for c0, c1 in ((0, S // 2), (S // 2, S)):
-            gather(1, 3, c0, c1)
-            interleave(nc.scalar.copy, 1, c0, c1)
-        for i in range(4):
-            gather(2, i, 0, S)
-            if i == 1:
-                nc.vector.quantize_mx(
-                    out=front_codes[:].bitcast(FP8X4),
-                    scales=front_scales[:],
-                    in_=front_packed[:].rearrange("p c t -> p (c t)"),
-                )
-        interleave(nc.scalar.copy, 2, 0, S)
-        for a in range(2):
-            for c0, c1 in BANKS:
-                multiply(a, c0, c1, False)
-        for i in range(3):
-            gather(LAST, i, 0, S - Q)
+            gather(LAST, i, 0, S)
         for c0, c1 in ((0, Q), (Q, S - Q)):
             gather(LAST, 3, c0, c1)
             interleave(nc.scalar.copy, LAST, c0, c1)
-        picked["end"] = keep.tile([P, 4, Q], F32, name="picked_end", tag="first", align_bytes=64)
-        for i in range(4):
-            gather(LAST, i, S - Q, S)
-        interleave(nc.scalar.copy, LAST, S - Q, S)
-        scales[2] = keep.tile([P, S], U8, name="scales2", tag="picked_last", align_bytes=64)[:]
+        front_scales = late.tile([P, 2 * S], U8, name="front_scales", align_bytes=64, offset=0)
+        scales[0] = front_scales[:, 0:S]
+        scales[1] = front_scales[:, S : 2 * S]
+        for a in range(2):
+            quantize(a, 0, S)
+            for c0, c1 in BANKS:
+                multiply(a, c0, c1, False)
+        for c0, c1 in ((S - Q, S),):
+            gather(LAST, 3, c0, c1)
+            interleave(nc.scalar.copy, LAST, c0, c1)
+        scales[2] = late.tile([P, S], U8, name="scales2", align_bytes=64, offset=1024)[:]
         quantize(LAST, 0, Q)
         multiply(LAST, *BANKS[0], False)
         quantize(2, 0, S // 2)
@@ -158,6 +146,6 @@ def tile_list_heads_res_kernel(tc, xT, w_words, w_scales, wgt, r, offs, out):
         multiply(2, *BANKS[3], False)
         quantize(LAST, S - Q, S)
         multiply(LAST, *BANKS[3], True)
-        done = keep.tile([M, S], F32, name="done", tag="first", align_bytes=64)
+        done = keep.tile([M, S], F32, name="done", tag="picked_last")
         for c0, c1 in BANKS:
             finish(c0, c1)

@@ -17,8 +17,13 @@ MULT, ADD = mybir.AluOpType.mult, mybir.AluOpType.add
 P = 128
 PASSES = K // 512
 LAST = PASSES - 1
-Q = 128
-BANKS = [(0, 128), (128, 256), (256, 384), (384, 512)]
+Q = S // 4
+BANKS = [(b * Q, (b + 1) * Q) for b in range(4)]
+MX_ALIGN = 64
+DMA_ALIGN = 256
+
+FIRST_AT = 2 * S - 2 * Q
+SCALES2_AT = 2 * S
 
 
 def tile_list_heads_res_kernel(tc, xT, w_words, w_scales, wgt, r, offs, out):
@@ -29,8 +34,8 @@ def tile_list_heads_res_kernel(tc, xT, w_words, w_scales, wgt, r, offs, out):
         psum = ctx.enter_context(tc.psum_pool(name="psum", bufs=1))
 
         lists = keep.tile([P, S // 16], U16, name="lists")
-        first = late.tile([P, Q], F32, name="first", align_bytes=64, offset=768)
-        factors = keep.tile([P, S], F32, name="factors")
+        first = late.tile([P, Q], F32, name="first", align_bytes=DMA_ALIGN, offset=FIRST_AT)
+        factors = keep.tile([P, S], F32, name="factors", align_bytes=DMA_ALIGN)
         nc.scalar.dma_start(out=first[:], in_=wgt[:, 0:Q])
         nc.scalar.copy(out=factors[:, 0:Q], in_=first[:])
 
@@ -38,38 +43,38 @@ def tile_list_heads_res_kernel(tc, xT, w_words, w_scales, wgt, r, offs, out):
         for a in range(PASSES):
             rows = xT[512 * a : 512 * (a + 1), :].rearrange("(p i) t -> p i t", i=4)
             for i in range(4):
-                planes[a, i] = keep.tile([P, T], F32, name=f"plane{a}_{i}")
+                planes[a, i] = keep.tile([P, T], F32, name=f"plane{a}_{i}", align_bytes=DMA_ALIGN)
                 nc.sync.dma_start(out=planes[a, i][:], in_=rows[:, i, :])
                 if a == 0 and i == 0:
                     nc.sync.dma_start(lists[:], offs)
                     nc.sync.dma_start(out=factors[:, Q:S], in_=wgt[:, Q:S])
 
-        w_s = keep.tile([P, PASSES, M], U8, name="w_s", align_bytes=64)
+        w_s = keep.tile([P, PASSES, M], U8, name="w_s", align_bytes=MX_ALIGN)
         nc.vector.memset(w_s[:].rearrange("p a n -> p (a n)").bitcast(I32), 0)
         for q in range(4):
             nc.sync.dma_start(
                 out=w_s[32 * q : 32 * q + 4, :, :].bitcast(I32),
                 in_=w_scales[:, 4 * q : 4 * q + 4, :].rearrange("a q n -> q a n").bitcast(I32),
             )
-        w_c = keep.tile([P, PASSES, M], U32, name="w_c", align_bytes=64)
+        w_c = keep.tile([P, PASSES, M], U32, name="w_c", align_bytes=DMA_ALIGN)
         nc.sync.dma_start(
             out=w_c[:].bitcast(I32),
             in_=w_words.rearrange("a p n t -> p a (n t)").bitcast(I32),
         )
-        res = keep.tile([P, S], F32, name="res")
+        res = keep.tile([P, S], F32, name="res", align_bytes=DMA_ALIGN)
         nc.sync.dma_start(out=res[:], in_=r)
 
         picked = {a: keep.tile([P, 4, S], F32, name=f"picked{a}") for a in range(LAST)}
-        front_packed = keep.tile([P, 2 * S, 4], BF16, name="front_packed", align_bytes=64)
-        front_codes = keep.tile([P, 2 * S], U32, name="front_codes", align_bytes=64)
-        picked[LAST] = keep.tile([P, 4, S], F32, name="picked_last", tag="picked_last")
+        front_packed = keep.tile([P, 2 * S, 4], BF16, name="front_packed", align_bytes=MX_ALIGN)
+        front_codes = keep.tile([P, 2 * S], U32, name="front_codes", align_bytes=MX_ALIGN)
+        picked[LAST] = keep.tile([P, 4, S], F32, name="picked_last", tag="picked_last", align_bytes=DMA_ALIGN)
         packed = {0: front_packed[:, 0:S, :], 1: front_packed[:, S : 2 * S, :]}
         codes = {0: front_codes[:, 0:S], 1: front_codes[:, S : 2 * S]}
         scales = {}
-        for a in (2, 3):
-            packed[a] = keep.tile([P, S, 4], BF16, name=f"packed{a}", align_bytes=64)[:]
-            codes[a] = keep.tile([P, S], U32, name=f"codes{a}", align_bytes=64)[:]
-        scales[3] = keep.tile([P, S], U8, name="scales3", align_bytes=64)[:]
+        for a in (2, LAST):
+            packed[a] = keep.tile([P, S, 4], BF16, name=f"packed{a}", align_bytes=MX_ALIGN)[:]
+            codes[a] = keep.tile([P, S], U32, name=f"codes{a}", align_bytes=MX_ALIGN)[:]
+        scales[LAST] = keep.tile([P, S], U8, name="scales3", align_bytes=MX_ALIGN)[:]
         acc = {c0: psum.tile([M, c1 - c0], F32, name=f"acc{c0}") for c0, c1 in BANKS}
 
         def gather(a, i, c0, c1):
@@ -80,20 +85,21 @@ def tile_list_heads_res_kernel(tc, xT, w_words, w_scales, wgt, r, offs, out):
                 MULT,
             )
 
-        def interleave(copy, a, c0, c1):
-            copy(
-                out=packed[a][:, c0:c1, :].rearrange("p (c i) t -> p c t i", i=4),
-                in_=picked[a][:, :, c0:c1].rearrange("p t (c i) -> p c t i", i=4),
+        def interleave(a, c0, c1):
+            nc.scalar.copy(
+                out=packed[a][:, c0:c1, :].rearrange("p (c n) i -> p c i n", n=4),
+                in_=picked[a][:, :, c0:c1].rearrange("p i (c n) -> p c i n", n=4),
             )
 
         def quantize(a, c0, c1):
             nc.vector.quantize_mx(
                 out=codes[a][:, c0:c1].bitcast(FP8X4),
                 scales=scales[a][:, c0:c1],
-                in_=packed[a][:, c0:c1, :].rearrange("p c t -> p (c t)"),
+                in_=packed[a][:, c0:c1, :].rearrange("p c i -> p (c i)"),
             )
 
-        def multiply(a, c0, c1, stop):
+        def multiply(a, b, closes=False):
+            c0, c1 = BANKS[b]
             nc.tensor.matmul_mx(
                 out=acc[c0][:],
                 lhsT=w_c[:, a, :].bitcast(FP8X4),
@@ -101,51 +107,50 @@ def tile_list_heads_res_kernel(tc, xT, w_words, w_scales, wgt, r, offs, out):
                 rhs=codes[a][:, c0:c1].bitcast(FP8X4),
                 rhs_scale=scales[a][:, c0:c1],
                 start=(a == 0),
-                stop=stop,
+                stop=closes,
             )
-
-        def finish(c0, c1):
-            nc.vector.tensor_tensor(done[:, c0:c1], acc[c0][:], res[:, c0:c1], ADD)
-            nc.sync.dma_start(out=out[:, c0:c1], in_=done[:, c0:c1])
 
         gather(0, 0, 0, Q)
         gather(0, 0, Q, S)
         for i in range(1, 4):
             gather(0, i, 0, S)
-        interleave(nc.scalar.copy, 0, 0, S)
+        interleave(0, 0, S)
         for a in (1, 2):
             for i in range(4):
                 gather(a, i, 0, S)
-            interleave(nc.scalar.copy, a, 0, S)
+            interleave(a, 0, S)
         for i in range(3):
             gather(LAST, i, 0, S)
+
         for c0, c1 in ((0, Q), (Q, S - Q)):
             gather(LAST, 3, c0, c1)
-            interleave(nc.scalar.copy, LAST, c0, c1)
-        front_scales = late.tile([P, 2 * S], U8, name="front_scales", align_bytes=64, offset=0)
+            interleave(LAST, c0, c1)
+        front_scales = late.tile([P, 2 * S], U8, name="front_scales", align_bytes=MX_ALIGN, offset=0)
         scales[0] = front_scales[:, 0:S]
         scales[1] = front_scales[:, S : 2 * S]
         for a in range(2):
             quantize(a, 0, S)
-            for c0, c1 in BANKS:
-                multiply(a, c0, c1, False)
-        for c0, c1 in ((S - Q, S),):
-            gather(LAST, 3, c0, c1)
-            interleave(nc.scalar.copy, LAST, c0, c1)
-        scales[2] = late.tile([P, S], U8, name="scales2", align_bytes=64, offset=1024)[:]
+            for b in range(4):
+                multiply(a, b)
+        gather(LAST, 3, S - Q, S)
+        interleave(LAST, S - Q, S)
+
+        scales[2] = late.tile([P, S], U8, name="scales2", align_bytes=MX_ALIGN, offset=SCALES2_AT)[:]
         quantize(LAST, 0, Q)
-        multiply(LAST, *BANKS[0], False)
-        quantize(2, 0, S // 2)
-        multiply(2, *BANKS[0], True)
-        multiply(2, *BANKS[1], False)
-        quantize(LAST, Q, S - Q)
-        multiply(LAST, *BANKS[1], True)
-        multiply(LAST, *BANKS[2], False)
-        quantize(2, S // 2, S)
-        multiply(2, *BANKS[2], True)
-        multiply(2, *BANKS[3], False)
-        quantize(LAST, S - Q, S)
-        multiply(LAST, *BANKS[3], True)
-        done = keep.tile([M, S], F32, name="done", tag="picked_last")
+        multiply(LAST, 0)
+        quantize(2, 0, 2 * Q)
+        multiply(2, 0, closes=True)
+        multiply(2, 1)
+        quantize(LAST, Q, 3 * Q)
+        multiply(LAST, 1, closes=True)
+        multiply(LAST, 2)
+        quantize(2, 2 * Q, S)
+        multiply(2, 2, closes=True)
+        multiply(2, 3)
+        quantize(LAST, 3 * Q, S)
+        multiply(LAST, 3, closes=True)
+
+        done = keep.tile([M, S], F32, name="done", tag="picked_last", align_bytes=DMA_ALIGN)
         for c0, c1 in BANKS:
-            finish(c0, c1)
+            nc.vector.tensor_tensor(done[:, c0:c1], acc[c0][:], res[:, c0:c1], ADD)
+            nc.sync.dma_start(out=out[:, c0:c1], in_=done[:, c0:c1])

@@ -25,17 +25,22 @@ DMA_ALIGN = 256
 FIRST_AT = 2 * S - 2 * Q
 SCALES2_AT = 2 * S
 
+KIB = 1024
+REGION = 64 * KIB
+PICKED_AT = [32 * KIB, 96 * KIB, 160 * KIB, 208 * KIB]
+
 
 def tile_list_heads_res_kernel(tc, xT, w_words, w_scales, wgt, r, offs, out):
     nc = tc.nc
     with ExitStack() as ctx:
         keep = ctx.enter_context(tc.tile_pool(name="keep", bufs=1))
         late = ctx.enter_context(tc.tile_pool(name="late", bufs=1))
+        wide = ctx.enter_context(tc.tile_pool(name="wide", bufs=1))
         psum = ctx.enter_context(tc.psum_pool(name="psum", bufs=1))
 
         lists = keep.tile([P, S // 16], U16, name="lists")
         first = late.tile([P, Q], F32, name="first", align_bytes=DMA_ALIGN, offset=FIRST_AT)
-        factors = keep.tile([P, S], F32, name="factors", align_bytes=DMA_ALIGN)
+        factors = wide.tile([P, S], F32, name="factors", align_bytes=DMA_ALIGN, offset=48 * KIB)
         nc.scalar.dma_start(out=first[:], in_=wgt[:, 0:Q])
         nc.scalar.copy(out=factors[:, 0:Q], in_=first[:])
 
@@ -43,7 +48,7 @@ def tile_list_heads_res_kernel(tc, xT, w_words, w_scales, wgt, r, offs, out):
         for a in range(PASSES):
             rows = xT[512 * a : 512 * (a + 1), :].rearrange("(p i) t -> p i t", i=4)
             for i in range(4):
-                planes[a, i] = keep.tile([P, T], F32, name=f"plane{a}_{i}", align_bytes=DMA_ALIGN)
+                planes[a, i] = wide.tile([P, T], F32, name=f"plane{a}_{i}", align_bytes=DMA_ALIGN, offset=i * REGION + a * 4 * T)
                 nc.sync.dma_start(out=planes[a, i][:], in_=rows[:, i, :])
                 if a == 0 and i == 0:
                     nc.sync.dma_start(lists[:], offs)
@@ -64,15 +69,14 @@ def tile_list_heads_res_kernel(tc, xT, w_words, w_scales, wgt, r, offs, out):
         res = keep.tile([P, S], F32, name="res", align_bytes=DMA_ALIGN)
         nc.sync.dma_start(out=res[:], in_=r)
 
-        picked = {a: keep.tile([P, 4, S], F32, name=f"picked{a}") for a in range(LAST)}
-        front_packed = keep.tile([P, 2 * S, 4], BF16, name="front_packed", align_bytes=MX_ALIGN)
+        picked = {a: wide.tile([P, 4, S], F32, name=f"picked{a}", offset=PICKED_AT[a]) for a in range(PASSES)}
+        front_packed = wide.tile([P, 2 * S, 4], BF16, name="front_packed", align_bytes=MX_ALIGN, offset=112 * KIB)
         front_codes = keep.tile([P, 2 * S], U32, name="front_codes", align_bytes=MX_ALIGN)
-        picked[LAST] = keep.tile([P, 4, S], F32, name="picked_last", tag="picked_last", align_bytes=DMA_ALIGN)
         packed = {0: front_packed[:, 0:S, :], 1: front_packed[:, S : 2 * S, :]}
         codes = {0: front_codes[:, 0:S], 1: front_codes[:, S : 2 * S]}
         scales = {}
         for a in (2, LAST):
-            packed[a] = keep.tile([P, S, 4], BF16, name=f"packed{a}", align_bytes=MX_ALIGN)[:]
+            packed[a] = wide.tile([P, S, 4], BF16, name=f"packed{a}", align_bytes=MX_ALIGN, offset=(168 + 4 * a) * KIB)[:]
             codes[a] = keep.tile([P, S], U32, name=f"codes{a}", align_bytes=MX_ALIGN)[:]
         scales[LAST] = keep.tile([P, S], U8, name="scales3", align_bytes=MX_ALIGN)[:]
         acc = {c0: psum.tile([M, c1 - c0], F32, name=f"acc{c0}") for c0, c1 in BANKS}
@@ -150,7 +154,7 @@ def tile_list_heads_res_kernel(tc, xT, w_words, w_scales, wgt, r, offs, out):
         quantize(LAST, 3 * Q, S)
         multiply(LAST, 3, closes=True)
 
-        done = keep.tile([M, S], F32, name="done", tag="picked_last", align_bytes=DMA_ALIGN)
+        done = wide.tile([M, S], F32, name="done", align_bytes=DMA_ALIGN, offset=PICKED_AT[LAST])
         for c0, c1 in BANKS:
             nc.vector.tensor_tensor(done[:, c0:c1], acc[c0][:], res[:, c0:c1], ADD)
             nc.sync.dma_start(out=out[:, c0:c1], in_=done[:, c0:c1])

@@ -27,6 +27,7 @@ SCALES2_AT = 2 * S
 
 KIB = 1024
 REGION = 64 * KIB
+HALF_TURN = 128
 PICKED_AT = [32 * KIB, 96 * KIB, 160 * KIB, 208 * KIB]
 
 
@@ -69,7 +70,7 @@ def tile_list_heads_res_kernel(tc, xT, w_words, w_scales, wgt, r, offs, out):
         res = keep.tile([P, S], F32, name="res", align_bytes=DMA_ALIGN)
         nc.sync.dma_start(out=res[:], in_=r)
 
-        picked = {a: wide.tile([P, 4, S], F32, name=f"picked{a}", offset=PICKED_AT[a]) for a in range(PASSES)}
+        picked = {a: wide.tile([P, 4, S], F32, name=f"picked{a}", offset=PICKED_AT[a] + HALF_TURN) for a in range(PASSES)}
         front_packed = wide.tile([P, 2 * S, 4], BF16, name="front_packed", align_bytes=MX_ALIGN, offset=112 * KIB)
         front_codes = keep.tile([P, 2 * S], U32, name="front_codes", align_bytes=MX_ALIGN)
         packed = {0: front_packed[:, 0:S, :], 1: front_packed[:, S : 2 * S, :]}

@@ -28,6 +28,7 @@ SCALES2_AT = 2 * S
 KIB = 1024
 REGION = 64 * KIB
 HALF_TURN = 128
+ROW_PAD = 16
 PICKED_AT = [32 * KIB, 96 * KIB, 160 * KIB, 208 * KIB]
 
 
@@ -70,7 +71,7 @@ def tile_list_heads_res_kernel(tc, xT, w_words, w_scales, wgt, r, offs, out):
         res = keep.tile([P, S], F32, name="res", align_bytes=DMA_ALIGN)
         nc.sync.dma_start(out=res[:], in_=r)
 
-        picked = {a: wide.tile([P, 4, S], F32, name=f"picked{a}", offset=PICKED_AT[a] + HALF_TURN) for a in range(PASSES)}
+        picked = {a: wide.tile([P, 4, S + ROW_PAD], F32, name=f"picked{a}", offset=PICKED_AT[a] + HALF_TURN) for a in range(PASSES)}
         front_packed = wide.tile([P, 2 * S, 4], BF16, name="front_packed", align_bytes=MX_ALIGN, offset=112 * KIB)
         front_codes = keep.tile([P, 2 * S], U32, name="front_codes", align_bytes=MX_ALIGN)
         packed = {0: front_packed[:, 0:S, :], 1: front_packed[:, S : 2 * S, :]}
@@ -127,18 +128,19 @@ def tile_list_heads_res_kernel(tc, xT, w_words, w_scales, wgt, r, offs, out):
         for i in range(3):
             gather(LAST, i, 0, S)
 
-        for c0, c1 in ((0, Q), (Q, S - Q)):
-            gather(LAST, 3, c0, c1)
-            interleave(LAST, c0, c1)
+        gather(LAST, 3, 0, Q)
+        interleave(LAST, 0, Q)
+        gather(LAST, 3, Q, S)
+        interleave(LAST, Q, S - Q)
+        interleave(LAST, S - Q, S)
         front_scales = late.tile([P, 2 * S], U8, name="front_scales", align_bytes=MX_ALIGN, offset=0)
         scales[0] = front_scales[:, 0:S]
         scales[1] = front_scales[:, S : 2 * S]
         for a in range(2):
-            quantize(a, 0, S)
-            for b in range(4):
-                multiply(a, b)
-        gather(LAST, 3, S - Q, S)
-        interleave(LAST, S - Q, S)
+            for half in range(2):
+                quantize(a, half * 2 * Q, (half + 1) * 2 * Q)
+                multiply(a, 2 * half)
+                multiply(a, 2 * half + 1)
 
         scales[2] = late.tile([P, S], U8, name="scales2", align_bytes=MX_ALIGN, offset=SCALES2_AT)[:]
         quantize(LAST, 0, Q)

@@ -18,13 +18,10 @@ P = 128
 PASSES = K // 512
 LAST = PASSES - 1
 Q = S // 4
+H = S // 2
 BANKS = [(b * Q, (b + 1) * Q) for b in range(4)]
 MX_ALIGN = 64
 DMA_ALIGN = 256
-
-FIRST_AT = 2 * S - 2 * Q
-SCALES2_AT = 2 * S
-
 KIB = 1024
 REGION = 64 * KIB
 HALF_TURN = 128
@@ -32,29 +29,35 @@ ROW_PAD = 16
 PICKED_AT = [32 * KIB, 96 * KIB, 160 * KIB, 208 * KIB]
 
 
+def plane_at(a, i):
+    return i * REGION + a * 4 * T
+
+
 def tile_list_heads_res_kernel(tc, xT, w_words, w_scales, wgt, r, offs, out):
     nc = tc.nc
     with ExitStack() as ctx:
         keep = ctx.enter_context(tc.tile_pool(name="keep", bufs=1))
-        late = ctx.enter_context(tc.tile_pool(name="late", bufs=1))
         wide = ctx.enter_context(tc.tile_pool(name="wide", bufs=1))
         psum = ctx.enter_context(tc.psum_pool(name="psum", bufs=1))
 
         lists = keep.tile([P, S // 16], U16, name="lists")
-        first = late.tile([P, Q], F32, name="first", align_bytes=DMA_ALIGN, offset=FIRST_AT)
         factors = wide.tile([P, S], F32, name="factors", align_bytes=DMA_ALIGN, offset=48 * KIB)
-        nc.scalar.dma_start(out=first[:], in_=wgt[:, 0:Q])
-        nc.scalar.copy(out=factors[:, 0:Q], in_=first[:])
+        picked = {a: wide.tile([P, 4, S + ROW_PAD], F32, name=f"picked{a}", offset=PICKED_AT[a] + HALF_TURN) for a in range(PASSES)}
+        first = picked[LAST][:, 2, H:S]
+        nc.scalar.dma_start(out=first, in_=wgt[:, 0:H])
+        nc.scalar.copy(out=factors[:, 0:H], in_=first)
 
         planes = {}
+        rows = xT.rearrange("(a p i) t -> a i p t", a=PASSES, i=4)
         for a in range(PASSES):
-            rows = xT[512 * a : 512 * (a + 1), :].rearrange("(p i) t -> p i t", i=4)
             for i in range(4):
-                planes[a, i] = wide.tile([P, T], F32, name=f"plane{a}_{i}", align_bytes=DMA_ALIGN, offset=i * REGION + a * 4 * T)
-                nc.sync.dma_start(out=planes[a, i][:], in_=rows[:, i, :])
-                if a == 0 and i == 0:
-                    nc.sync.dma_start(lists[:], offs)
-                    nc.sync.dma_start(out=factors[:, Q:S], in_=wgt[:, Q:S])
+                planes[a, i] = wide.tile([P, T], F32, name=f"plane{a}_{i}", align_bytes=DMA_ALIGN, offset=plane_at(a, i))
+        nc.sync.dma_start(out=planes[0, 0][:], in_=rows[0, 0])
+        nc.sync.dma_start(lists[:], offs)
+        nc.sync.dma_start(out=factors[:, H:S], in_=wgt[:, H:S])
+        for n in range(1, 4 * PASSES):
+            a, i = divmod(n, 4)
+            nc.sync.dma_start(out=planes[a, i][:], in_=rows[a, i])
 
         w_s = keep.tile([P, PASSES, M], U8, name="w_s", align_bytes=MX_ALIGN)
         nc.vector.memset(w_s[:].rearrange("p a n -> p (a n)").bitcast(I32), 0)
@@ -71,23 +74,16 @@ def tile_list_heads_res_kernel(tc, xT, w_words, w_scales, wgt, r, offs, out):
         res = keep.tile([P, S], F32, name="res", align_bytes=DMA_ALIGN)
         nc.sync.dma_start(out=res[:], in_=r)
 
-        picked = {a: wide.tile([P, 4, S + ROW_PAD], F32, name=f"picked{a}", offset=PICKED_AT[a] + HALF_TURN) for a in range(PASSES)}
-        front_packed = wide.tile([P, 2 * S, 4], BF16, name="front_packed", align_bytes=MX_ALIGN, offset=112 * KIB)
-        front_codes = keep.tile([P, 2 * S], U32, name="front_codes", align_bytes=MX_ALIGN)
-        packed = {0: front_packed[:, 0:S, :], 1: front_packed[:, S : 2 * S, :]}
-        codes = {0: front_codes[:, 0:S], 1: front_codes[:, S : 2 * S]}
-        scales = {}
-        for a in (2, LAST):
-            packed[a] = wide.tile([P, S, 4], BF16, name=f"packed{a}", align_bytes=MX_ALIGN, offset=(168 + 4 * a) * KIB)[:]
-            codes[a] = keep.tile([P, S], U32, name=f"codes{a}", align_bytes=MX_ALIGN)[:]
-        scales[LAST] = keep.tile([P, S], U8, name="scales3", align_bytes=MX_ALIGN)[:]
+        packed = {a: wide.tile([P, S, 4], BF16, name=f"packed{a}", align_bytes=MX_ALIGN, offset=(112 + 4 * a) * KIB) for a in range(PASSES)}
+        codes = {a: keep.tile([P, S], U32, name=f"codes{a}", align_bytes=MX_ALIGN) for a in range(PASSES)}
+        scales = {LAST: keep.tile([P, S], U8, name="scales3", align_bytes=MX_ALIGN)}
         acc = {c0: psum.tile([M, c1 - c0], F32, name=f"acc{c0}") for c0, c1 in BANKS}
 
-        def gather(a, i, c0, c1):
+        def gather(a, i, c0, c1, weights=factors):
             nc.vector.tensor_tensor(
                 picked[a][:, i, c0:c1],
                 planes[a, i][:].indirect(lists[:, c0 // 16 : c1 // 16]),
-                first[:] if c1 == Q else factors[:, c0:c1],
+                weights[:, c0:c1],
                 MULT,
             )
 
@@ -97,10 +93,15 @@ def tile_list_heads_res_kernel(tc, xT, w_words, w_scales, wgt, r, offs, out):
                 in_=picked[a][:, :, c0:c1].rearrange("p i (c n) -> p c i n", n=4),
             )
 
+        def scale_bytes(a, c0, c1):
+            if (a, c0) == (2, 3 * Q):
+                return scales["end"][:]
+            return scales[a][:, c0:c1]
+
         def quantize(a, c0, c1):
             nc.vector.quantize_mx(
                 out=codes[a][:, c0:c1].bitcast(FP8X4),
-                scales=scales[a][:, c0:c1],
+                scales=scale_bytes(a, c0, c1),
                 in_=packed[a][:, c0:c1, :].rearrange("p c i -> p (c i)"),
             )
 
@@ -111,13 +112,13 @@ def tile_list_heads_res_kernel(tc, xT, w_words, w_scales, wgt, r, offs, out):
                 lhsT=w_c[:, a, :].bitcast(FP8X4),
                 lhsT_scale=w_s[:, a, :],
                 rhs=codes[a][:, c0:c1].bitcast(FP8X4),
-                rhs_scale=scales[a][:, c0:c1],
+                rhs_scale=scale_bytes(a, c0, c1),
                 start=(a == 0),
                 stop=closes,
             )
 
-        gather(0, 0, 0, Q)
-        gather(0, 0, Q, S)
+        gather(0, 0, 0, H, first)
+        gather(0, 0, H, S)
         for i in range(1, 4):
             gather(0, i, 0, S)
         interleave(0, 0, S)
@@ -125,37 +126,37 @@ def tile_list_heads_res_kernel(tc, xT, w_words, w_scales, wgt, r, offs, out):
             for i in range(4):
                 gather(a, i, 0, S)
             interleave(a, 0, S)
-        for i in range(3):
+        for i in range(2):
             gather(LAST, i, 0, S)
+        gather(LAST, 2, 0, H)
+        gather(LAST, 3, 0, H, first)
+        interleave(LAST, 0, H)
+        gather(LAST, 3, H, S)
+        gather(LAST, 2, H, S)
+        interleave(LAST, H, S)
 
-        gather(LAST, 3, 0, Q)
-        interleave(LAST, 0, Q)
-        gather(LAST, 3, Q, S)
-        interleave(LAST, Q, S - Q)
-        interleave(LAST, S - Q, S)
-        front_scales = late.tile([P, 2 * S], U8, name="front_scales", align_bytes=MX_ALIGN, offset=0)
-        scales[0] = front_scales[:, 0:S]
-        scales[1] = front_scales[:, S : 2 * S]
+        for a in range(LAST):
+            scales[a] = wide.tile([P, S], U8, name=f"scales{a}", align_bytes=MX_ALIGN, offset=plane_at(LAST, 3) + a * S)
         for a in range(2):
             for half in range(2):
-                quantize(a, half * 2 * Q, (half + 1) * 2 * Q)
+                quantize(a, half * H, (half + 1) * H)
                 multiply(a, 2 * half)
                 multiply(a, 2 * half + 1)
 
-        scales[2] = late.tile([P, S], U8, name="scales2", align_bytes=MX_ALIGN, offset=SCALES2_AT)[:]
-        quantize(LAST, 0, Q)
-        multiply(LAST, 0)
-        quantize(2, 0, 2 * Q)
-        multiply(2, 0, closes=True)
-        multiply(2, 1)
-        quantize(LAST, Q, 3 * Q)
-        multiply(LAST, 1, closes=True)
-        multiply(LAST, 2)
-        quantize(2, 2 * Q, S)
-        multiply(2, 2, closes=True)
-        multiply(2, 3)
-        quantize(LAST, 3 * Q, S)
-        multiply(LAST, 3, closes=True)
+        quantize(2, 0, Q)
+        multiply(2, 0)
+        quantize(LAST, 0, H)
+        multiply(LAST, 0, closes=True)
+        multiply(LAST, 1)
+        quantize(2, Q, 3 * Q)
+        multiply(2, 1, closes=True)
+        multiply(2, 2)
+        quantize(LAST, H, S)
+        multiply(LAST, 2, closes=True)
+        multiply(LAST, 3)
+        scales["end"] = wide.tile([P, Q], U8, name="scales_end", align_bytes=MX_ALIGN, offset=PICKED_AT[LAST] + 4 * KIB)
+        quantize(2, 3 * Q, S)
+        multiply(2, 3, closes=True)
 
         done = wide.tile([M, S], F32, name="done", align_bytes=DMA_ALIGN, offset=PICKED_AT[LAST])
         for c0, c1 in BANKS:

@@ -26,7 +26,9 @@ KIB = 1024
 REGION = 64 * KIB
 HALF_TURN = 128
 ROW_PAD = 16
-PICKED_AT = [32 * KIB, 96 * KIB, 160 * KIB, 208 * KIB]
+PICKED_AT = [32 * KIB, 96 * KIB, 160 * KIB, 176 * KIB]
+EARLY = 3 * Q
+LAST_PITCH = EARLY + 2 * H + ROW_PAD
 
 
 def plane_at(a, i):
@@ -42,10 +44,9 @@ def tile_list_heads_res_kernel(tc, xT, w_words, w_scales, wgt, r, offs, out):
 
         lists = keep.tile([P, S // 16], U16, name="lists")
         factors = wide.tile([P, S], F32, name="factors", align_bytes=DMA_ALIGN, offset=48 * KIB)
-        picked = {a: wide.tile([P, 4, S + ROW_PAD], F32, name=f"picked{a}", offset=PICKED_AT[a] + HALF_TURN) for a in range(PASSES)}
-        first = picked[LAST][:, 2, H:S]
-        nc.scalar.dma_start(out=first, in_=wgt[:, 0:H])
-        nc.scalar.copy(out=factors[:, 0:H], in_=first)
+        pitch = {0: S + ROW_PAD, 1: S + ROW_PAD, 2: S + ROW_PAD, LAST: LAST_PITCH}
+        picked = {a: wide.tile([P, 4, pitch[a]], F32, name=f"picked{a}", align_bytes=MX_ALIGN, offset=PICKED_AT[a] + HALF_TURN) for a in range(PASSES)}
+        nc.scalar.dma_start(out=factors[:, 0:Q], in_=wgt[:, 0:Q])
 
         planes = {}
         rows = xT.rearrange("(a p i) t -> a i p t", a=PASSES, i=4)
@@ -54,16 +55,16 @@ def tile_list_heads_res_kernel(tc, xT, w_words, w_scales, wgt, r, offs, out):
                 planes[a, i] = wide.tile([P, T], F32, name=f"plane{a}_{i}", align_bytes=DMA_ALIGN, offset=plane_at(a, i))
         nc.sync.dma_start(out=planes[0, 0][:], in_=rows[0, 0])
         nc.sync.dma_start(lists[:], offs)
-        nc.sync.dma_start(out=factors[:, H:S], in_=wgt[:, H:S])
+        nc.sync.dma_start(out=factors[:, Q:S], in_=wgt[:, Q:S])
         for n in range(1, 4 * PASSES):
             a, i = divmod(n, 4)
             nc.sync.dma_start(out=planes[a, i][:], in_=rows[a, i])
 
-        w_s = keep.tile([P, PASSES, M], U8, name="w_s", align_bytes=MX_ALIGN)
-        nc.vector.memset(w_s[:].rearrange("p a n -> p (a n)").bitcast(I32), 0)
+        shared = keep.tile([P, 2 * S], U8, name="shared", align_bytes=MX_ALIGN)
+        nc.vector.memset(shared[:].bitcast(I32), 0)
         for q in range(4):
             nc.sync.dma_start(
-                out=w_s[32 * q : 32 * q + 4, :, :].bitcast(I32),
+                out=shared[32 * q + 4 : 32 * q + 8, :].rearrange("q (a n) -> q a n", a=PASSES)[:, :, 0:M].bitcast(I32),
                 in_=w_scales[:, 4 * q : 4 * q + 4, :].rearrange("a q n -> q a n").bitcast(I32),
             )
         w_c = keep.tile([P, PASSES, M], U32, name="w_c", align_bytes=DMA_ALIGN)
@@ -74,35 +75,37 @@ def tile_list_heads_res_kernel(tc, xT, w_words, w_scales, wgt, r, offs, out):
         res = keep.tile([P, S], F32, name="res", align_bytes=DMA_ALIGN)
         nc.sync.dma_start(out=res[:], in_=r)
 
-        packed = {a: wide.tile([P, S, 4], BF16, name=f"packed{a}", align_bytes=MX_ALIGN, offset=(112 + 4 * a) * KIB) for a in range(PASSES)}
+        packed = {a: wide.tile([P, S, 4], BF16, name=f"packed{a}", align_bytes=MX_ALIGN, offset=(112 + 4 * a) * KIB) for a in range(1, PASSES)}
+        parked = [picked[LAST][:, 2 + half, EARLY : EARLY + 2 * H].bitcast(BF16).rearrange("p (c i) -> p c i", i=4) for half in range(2)]
+
+        def packed_at(a, c0, c1):
+            if a == 0:
+                return parked[c0 // H][:, c0 % H : c0 % H + c1 - c0, :]
+            return packed[a][:, c0:c1, :]
+
         codes = {a: keep.tile([P, S], U32, name=f"codes{a}", align_bytes=MX_ALIGN) for a in range(PASSES)}
-        scales = {LAST: keep.tile([P, S], U8, name="scales3", align_bytes=MX_ALIGN)}
+        scales = {0: shared[:, 0:S], 1: shared[:, S : 2 * S]}
         acc = {c0: psum.tile([M, c1 - c0], F32, name=f"acc{c0}") for c0, c1 in BANKS}
 
-        def gather(a, i, c0, c1, weights=factors):
+        def gather(a, i, c0, c1):
             nc.vector.tensor_tensor(
                 picked[a][:, i, c0:c1],
                 planes[a, i][:].indirect(lists[:, c0 // 16 : c1 // 16]),
-                weights[:, c0:c1],
+                factors[:, c0:c1],
                 MULT,
             )
 
         def interleave(a, c0, c1):
             nc.scalar.copy(
-                out=packed[a][:, c0:c1, :].rearrange("p (c n) i -> p c i n", n=4),
+                out=packed_at(a, c0, c1).rearrange("p (c n) i -> p c i n", n=4),
                 in_=picked[a][:, :, c0:c1].rearrange("p i (c n) -> p c i n", n=4),
             )
-
-        def scale_bytes(a, c0, c1):
-            if (a, c0) == (2, 3 * Q):
-                return scales["end"][:]
-            return scales[a][:, c0:c1]
 
         def quantize(a, c0, c1):
             nc.vector.quantize_mx(
                 out=codes[a][:, c0:c1].bitcast(FP8X4),
-                scales=scale_bytes(a, c0, c1),
-                in_=packed[a][:, c0:c1, :].rearrange("p c i -> p (c i)"),
+                scales=scales[a][:, c0:c1],
+                in_=packed_at(a, c0, c1).rearrange("p c i -> p (c i)"),
             )
 
         def multiply(a, b, closes=False):
@@ -110,53 +113,53 @@ def tile_list_heads_res_kernel(tc, xT, w_words, w_scales, wgt, r, offs, out):
             nc.tensor.matmul_mx(
                 out=acc[c0][:],
                 lhsT=w_c[:, a, :].bitcast(FP8X4),
-                lhsT_scale=w_s[:, a, :],
+                lhsT_scale=shared[4:P, a * H : a * H + M],
                 rhs=codes[a][:, c0:c1].bitcast(FP8X4),
-                rhs_scale=scale_bytes(a, c0, c1),
+                rhs_scale=scales[a][:, c0:c1],
                 start=(a == 0),
                 stop=closes,
             )
 
-        gather(0, 0, 0, H, first)
-        gather(0, 0, H, S)
+        gather(0, 0, 0, Q)
+        gather(0, 0, Q, S)
         for i in range(1, 4):
             gather(0, i, 0, S)
-        interleave(0, 0, S)
+        interleave(0, 0, H)
+        interleave(0, H, S)
         for a in (1, 2):
             for i in range(4):
                 gather(a, i, 0, S)
             interleave(a, 0, S)
         for i in range(2):
             gather(LAST, i, 0, S)
-        gather(LAST, 2, 0, H)
-        gather(LAST, 3, 0, H, first)
-        interleave(LAST, 0, H)
-        gather(LAST, 3, H, S)
-        gather(LAST, 2, H, S)
-        interleave(LAST, H, S)
-
-        for a in range(LAST):
-            scales[a] = wide.tile([P, S], U8, name=f"scales{a}", align_bytes=MX_ALIGN, offset=plane_at(LAST, 3) + a * S)
+        gather(LAST, 2, 0, EARLY)
+        gather(LAST, 3, 0, EARLY)
+        interleave(LAST, 0, Q)
+        interleave(LAST, Q, EARLY)
         for a in range(2):
             for half in range(2):
                 quantize(a, half * H, (half + 1) * H)
                 multiply(a, 2 * half)
                 multiply(a, 2 * half + 1)
+        gather(LAST, 2, EARLY, S)
+        gather(LAST, 3, EARLY, S)
+        interleave(LAST, EARLY, S)
 
-        quantize(2, 0, Q)
-        multiply(2, 0)
-        quantize(LAST, 0, H)
-        multiply(LAST, 0, closes=True)
-        multiply(LAST, 1)
-        quantize(2, Q, 3 * Q)
-        multiply(2, 1, closes=True)
-        multiply(2, 2)
-        quantize(LAST, H, S)
-        multiply(LAST, 2, closes=True)
-        multiply(LAST, 3)
-        scales["end"] = wide.tile([P, Q], U8, name="scales_end", align_bytes=MX_ALIGN, offset=PICKED_AT[LAST] + 4 * KIB)
-        quantize(2, 3 * Q, S)
-        multiply(2, 3, closes=True)
+        for a in (2, LAST):
+            scales[a] = wide.tile([P, S], U8, name=f"scales{a}", align_bytes=MX_ALIGN, offset=plane_at(LAST, 2) + a * S)
+        quantize(LAST, 0, Q)
+        multiply(LAST, 0)
+        quantize(2, 0, H)
+        multiply(2, 0, closes=True)
+        multiply(2, 1)
+        quantize(LAST, Q, 3 * Q)
+        multiply(LAST, 1, closes=True)
+        multiply(LAST, 2)
+        quantize(2, H, S)
+        multiply(2, 2, closes=True)
+        multiply(2, 3)
+        quantize(LAST, 3 * Q, S)
+        multiply(LAST, 3, closes=True)
 
         done = wide.tile([M, S], F32, name="done", align_bytes=DMA_ALIGN, offset=PICKED_AT[LAST])
         for c0, c1 in BANKS:

from contextlib import ExitStack

import concourse.mybir as mybir

K, M, T, S = 2048, 128, 1024, 512
FLOPS = 2 * K * M * S

F32 = mybir.dt.float32
BF16 = mybir.dt.bfloat16
I32 = mybir.dt.int32
U32 = mybir.dt.uint32
U16 = mybir.dt.uint16
U8 = mybir.dt.uint8
FP8X4 = mybir.dt.float8_e4m3fn_x4
MULT, ADD = mybir.AluOpType.mult, mybir.AluOpType.add

P = 128
PASSES = K // 512
LAST = PASSES - 1
Q = S // 4
H = S // 2
BANKS = [(b * Q, (b + 1) * Q) for b in range(4)]
MX_ALIGN = 64
DMA_ALIGN = 256
KIB = 1024
REGION = 64 * KIB
HALF_TURN = 128
ROW_PAD = 16
PICKED_AT = [32 * KIB, 96 * KIB, 160 * KIB, 176 * KIB]
EARLY = 3 * Q
LAST_PITCH = EARLY + 2 * H + ROW_PAD


def plane_at(a, i):
    return i * REGION + a * 4 * T


def tile_list_heads_res_kernel(tc, xT, w_words, w_scales, wgt, r, offs, out):
    nc = tc.nc
    with ExitStack() as ctx:
        keep = ctx.enter_context(tc.tile_pool(name="keep", bufs=1))
        wide = ctx.enter_context(tc.tile_pool(name="wide", bufs=1))
        psum = ctx.enter_context(tc.psum_pool(name="psum", bufs=1))

        lists = keep.tile([P, S // 16], U16, name="lists")
        factors = wide.tile([P, S], F32, name="factors", align_bytes=DMA_ALIGN, offset=48 * KIB)
        pitch = {0: S + ROW_PAD, 1: S + ROW_PAD, 2: S + ROW_PAD, LAST: LAST_PITCH}
        picked = {a: wide.tile([P, 4, pitch[a]], F32, name=f"picked{a}", align_bytes=MX_ALIGN, offset=PICKED_AT[a] + HALF_TURN) for a in range(PASSES)}
        nc.scalar.dma_start(out=factors[:, 0:Q], in_=wgt[:, 0:Q])

        planes = {}
        rows = xT.rearrange("(a p i) t -> a i p t", a=PASSES, i=4)
        for a in range(PASSES):
            for i in range(4):
                planes[a, i] = wide.tile([P, T], F32, name=f"plane{a}_{i}", align_bytes=DMA_ALIGN, offset=plane_at(a, i))
        nc.sync.dma_start(out=planes[0, 0][:], in_=rows[0, 0])
        nc.sync.dma_start(lists[:], offs)
        nc.sync.dma_start(out=factors[:, Q:S], in_=wgt[:, Q:S])
        for n in range(1, 4 * PASSES):
            a, i = divmod(n, 4)
            nc.sync.dma_start(out=planes[a, i][:], in_=rows[a, i])

        shared = keep.tile([P, 2 * S], U8, name="shared", align_bytes=MX_ALIGN)
        nc.vector.memset(shared[:].bitcast(I32), 0)
        for q in range(4):
            nc.sync.dma_start(
                out=shared[32 * q + 4 : 32 * q + 8, :].rearrange("q (a n) -> q a n", a=PASSES)[:, :, 0:M].bitcast(I32),
                in_=w_scales[:, 4 * q : 4 * q + 4, :].rearrange("a q n -> q a n").bitcast(I32),
            )
        w_c = keep.tile([P, PASSES, M], U32, name="w_c", align_bytes=DMA_ALIGN)
        nc.sync.dma_start(
            out=w_c[:].bitcast(I32),
            in_=w_words.rearrange("a p n t -> p a (n t)").bitcast(I32),
        )
        res = keep.tile([P, S], F32, name="res", align_bytes=DMA_ALIGN)
        nc.sync.dma_start(out=res[:], in_=r)

        packed = {a: wide.tile([P, S, 4], BF16, name=f"packed{a}", align_bytes=MX_ALIGN, offset=(112 + 4 * a) * KIB) for a in range(1, PASSES)}
        parked = [picked[LAST][:, 2 + half, EARLY : EARLY + 2 * H].bitcast(BF16).rearrange("p (c i) -> p c i", i=4) for half in range(2)]

        def packed_at(a, c0, c1):
            if a == 0:
                return parked[c0 // H][:, c0 % H : c0 % H + c1 - c0, :]
            return packed[a][:, c0:c1, :]

        codes = {a: keep.tile([P, S], U32, name=f"codes{a}", align_bytes=MX_ALIGN) for a in range(PASSES)}
        scales = {0: shared[:, 0:S], 1: shared[:, S : 2 * S]}
        acc = {c0: psum.tile([M, c1 - c0], F32, name=f"acc{c0}") for c0, c1 in BANKS}

        def gather(a, i, c0, c1):
            nc.vector.tensor_tensor(
                picked[a][:, i, c0:c1],
                planes[a, i][:].indirect(lists[:, c0 // 16 : c1 // 16]),
                factors[:, c0:c1],
                MULT,
            )

        def interleave(a, c0, c1):
            nc.scalar.copy(
                out=packed_at(a, c0, c1).rearrange("p (c n) i -> p c i n", n=4),
                in_=picked[a][:, :, c0:c1].rearrange("p i (c n) -> p c i n", n=4),
            )

        def quantize(a, c0, c1):
            nc.vector.quantize_mx(
                out=codes[a][:, c0:c1].bitcast(FP8X4),
                scales=scales[a][:, c0:c1],
                in_=packed_at(a, c0, c1).rearrange("p c i -> p (c i)"),
            )

        def multiply(a, b, closes=False):
            c0, c1 = BANKS[b]
            nc.tensor.matmul_mx(
                out=acc[c0][:],
                lhsT=w_c[:, a, :].bitcast(FP8X4),
                lhsT_scale=shared[4:P, a * H : a * H + M],
                rhs=codes[a][:, c0:c1].bitcast(FP8X4),
                rhs_scale=scales[a][:, c0:c1],
                start=(a == 0),
                stop=closes,
            )

        gather(0, 0, 0, Q)
        gather(0, 0, Q, S)
        for i in range(1, 4):
            gather(0, i, 0, S)
        interleave(0, 0, H)
        interleave(0, H, S)
        for a in (1, 2):
            for i in range(4):
                gather(a, i, 0, S)
            interleave(a, 0, S)
        for i in range(2):
            gather(LAST, i, 0, S)
        gather(LAST, 2, 0, EARLY)
        gather(LAST, 3, 0, EARLY)
        interleave(LAST, 0, Q)
        interleave(LAST, Q, EARLY)
        for a in range(2):
            for half in range(2):
                quantize(a, half * H, (half + 1) * H)
                multiply(a, 2 * half)
                multiply(a, 2 * half + 1)
        gather(LAST, 2, EARLY, S)
        gather(LAST, 3, EARLY, S)
        interleave(LAST, EARLY, S)

        for a in (2, LAST):
            scales[a] = wide.tile([P, S], U8, name=f"scales{a}", align_bytes=MX_ALIGN, offset=plane_at(LAST, 2) + a * S)
        quantize(LAST, 0, Q)
        multiply(LAST, 0)
        quantize(2, 0, H)
        multiply(2, 0, closes=True)
        multiply(2, 1)
        quantize(LAST, Q, 3 * Q)
        multiply(LAST, 1, closes=True)
        multiply(LAST, 2)
        quantize(2, H, S)
        multiply(2, 2, closes=True)
        multiply(2, 3)
        quantize(LAST, 3 * Q, S)
        multiply(LAST, 3, closes=True)

        done = wide.tile([M, S], F32, name="done", align_bytes=DMA_ALIGN, offset=PICKED_AT[LAST])
        for c0, c1 in BANKS:
            nc.vector.tensor_tensor(done[:, c0:c1], acc[c0][:], res[:, c0:c1], ADD)
            nc.sync.dma_start(out=out[:, c0:c1], in_=done[:, c0:c1])
